import numpy as np
import ml_dtypes


def mxq(x, axis, fmt="e4m3"):
    dtype, down = {"e4m3": (ml_dtypes.float8_e4m3fn, 7), "e5m2": (ml_dtypes.float8_e5m2, 14)}[fmt]
    v = np.moveaxis(np.asarray(x, np.float32).astype(ml_dtypes.bfloat16).astype(np.float64), axis, -1)
    blocks = v.reshape(v.shape[:-1] + (-1, 32))
    amax = np.abs(blocks).max(-1, keepdims=True)
    byte = np.maximum(np.where(amax > 0, np.frexp(amax)[1] - 1 + 127, 0) - down, 1)
    scale = np.exp2(byte - 127.0)
    codes = (blocks / scale).astype(np.float32).astype(dtype).astype(np.float64)
    return np.moveaxis((codes * scale).reshape(v.shape), -1, axis)


WIDE = False


def mx_kscale(k):
    if not WIDE:
        return np.ones(k)
    levels = np.array([10, -10, 5, -5, 0])
    if k % 512:
        return np.exp2(np.random.permutation(np.resize(levels, k // 32))).repeat(32)
    a = np.empty((k // 512, 16))
    for p in range(k // 512):
        a[p, :8] = np.random.permutation(np.resize(levels, 8))
        for g in range(8):
            far = levels[np.abs(levels - a[p, g]) >= 10]
            a[p, g + 8] = far[np.random.randint(len(far))]
    return np.exp2(a.ravel()).repeat(32)


BF16 = ml_dtypes.bfloat16


def bf(x):
    return np.asarray(x, np.float32).astype(BF16)


def f64(x):
    return np.asarray(x).astype(np.float64)


E2M1 = np.array([0.0, 0.5, 1.0, 1.5, 2.0, 3.0, 4.0, 6.0, -0.0, -0.5, -1.0, -1.5, -2.0, -3.0, -4.0, -6.0])


def pack_weight(w, fmt):
    k, n = w.shape
    w = f64(bf(w)).reshape(k // 32, 32, n)
    amax = np.abs(w).max(1)
    if fmt == "e4m3":
        byte = np.frexp(amax)[1] - 1 + 127 - 7
    else:
        mant, ex = np.frexp(amax / 6.0)
        byte = np.where(mant > 0.5, ex, ex - 1) + 127
    byte = np.clip(np.where(amax > 0, byte, 1), 1, 254)
    scaled = (w * np.exp2(127.0 - byte)[:, None, :]).reshape(k, n).astype(np.float32)
    by_word = np.ascontiguousarray(scaled.reshape(k // 512, 128, 4, n).transpose(0, 1, 3, 2))
    if fmt == "e4m3":
        words = by_word.astype(ml_dtypes.float8_e4m3fn).view(np.uint8)
    else:
        c = by_word.astype(ml_dtypes.float4_e2m1fn).view(np.uint8) & 0xF
        words = c[..., 0::2] | (c[..., 1::2] << 4)
    return np.ascontiguousarray(words), np.ascontiguousarray(byte.astype(np.uint8).reshape(k // 512, 16, n))


def unpack_weight(words, scales, fmt):
    g, p, n, _ = words.shape
    if fmt == "e4m3":
        vals = np.ascontiguousarray(words).view(ml_dtypes.float8_e4m3fn).astype(np.float64)
    else:
        nib = np.empty((g, p, n, 4), np.uint8)
        nib[..., 0::2] = words & 0xF
        nib[..., 1::2] = words >> 4
        vals = E2M1[nib]
    vals = vals * np.repeat(np.exp2(scales.astype(np.float64) - 127.0), 8, axis=1)[..., None]
    return vals.transpose(0, 1, 3, 2).reshape(g * 512, n)
def pack4(w):
    words, scales = pack_weight(w, "e2m1")
    return words.reshape(words.shape[0], 128, -1), scales


def unpack4(words, scales):
    return unpack_weight(words.reshape(words.shape[0], 128, -1, 2), scales, "e2m1")


M, D, F, C = 1024, 1024, 2048, 512


def draw0():
    s = mx_kscale(D)
    t = mx_kscale(F)
    u = mx_kscale(M)
    x = np.random.standard_normal((M, D)) * s
    w_enc = np.random.standard_normal((D, F)) / np.sqrt(D) / s[:, None] * t
    b = 0.2 * np.random.standard_normal(F) * t
    norms = np.exp(0.3 * np.random.standard_normal(M)) * u
    w_dec = np.random.standard_normal((F, D)) / np.sqrt(F) / t[:, None]
    concepts = np.random.standard_normal((M, C)) / np.sqrt(M) / u[:, None]
    dec_words, dec_scales = pack4(w_dec)
    return {"x": bf(x), "w_enc": bf(w_enc), "b": bf(b), "norms": bf(norms),
            "dec_words": dec_words, "dec_scales": dec_scales,
            "concepts": bf(concepts)}


def core(x, w_enc, b, norms, dec_words, dec_scales, concepts):
    z = mxq(f64(x), 1, "e4m3") @ mxq(f64(w_enc), 0, "e4m3")
    h = np.maximum(z + f64(b), 0.0) * f64(norms)[:, None]
    recon = mxq(h, 1, "e4m3") @ unpack4(dec_words, dec_scales)
    assoc = mxq(h, 0, "e4m3").T @ mxq(f64(concepts), 0, "e4m3")
    return recon, assoc


def e4m3fn_bytes(y):
    return np.clip(np.asarray(y, np.float64), -448.0, 448.0).astype(np.float32).astype(ml_dtypes.float8_e4m3fn).view(np.uint8)


def e4m3fn_values(b):
    return np.asarray(b, np.uint8).view(ml_dtypes.float8_e4m3fn).astype(np.float64)


def setup_inputs():
    d = draw0()
    x0 = np.asarray(d['x']).astype(np.float64)
    s = (np.max(np.abs(x0), axis=(0,), keepdims=True) / 448.0).astype(np.float32)
    out = {}
    for k, v in d.items():
        if k == 'x':
            out['x_bytes'] = e4m3fn_bytes(x0 / s.astype(np.float64))
            out['x_scale'] = s
        else:
            out[k] = v
    return out


def reference(x_bytes, x_scale, w_enc, b, norms, dec_words, dec_scales, concepts):
    return core(e4m3fn_values(x_bytes) * x_scale.astype(np.float64), w_enc, b, norms, dec_words, dec_scales, concepts)

@@ -1,0 +1,547 @@
+from contextlib import ExitStack
+
+import concourse.mybir as mybir
+from concourse.masks import make_identity
+
+F32 = mybir.dt.float32
+BF16 = mybir.dt.bfloat16
+I32 = mybir.dt.int32
+U32 = mybir.dt.uint32
+U8 = mybir.dt.uint8
+FP8 = mybir.dt.float8_e4m3fn
+FP8X4 = mybir.dt.float8_e4m3fn_x4
+FP4X4 = mybir.dt.float4_e2m1fn_x4
+ALU = mybir.AluOpType
+ACT = mybir.ActivationFunctionType
+
+M, D, F, C = 1024, 1024, 2048, 512
+P = 128
+Z_BANKS, T_BANKS, O_BANKS = 3, 2, 3
+FLOPS = 2 * (2 * M * D * F + F * M * C)
+
+
+def tile_sae_decode_concepts_s8_kernel(
+    tc, x_bytes, x_scale, w_enc, b, norms, dec_words, dec_scales, concepts, out_0, out_1
+):
+    nc = tc.nc
+    with ExitStack() as ctx:
+        one = ctx.enter_context(tc.tile_pool(name="one", bufs=1))
+        roll = ctx.enter_context(tc.tile_pool(name="roll", bufs=2))
+        psum = ctx.enter_context(tc.psum_pool(name="psum", bufs=2))
+
+        ident = one.tile([P, P], F32, name="ident")
+        make_identity(nc, ident[:])
+        ident_bf = one.tile([P, P], BF16, name="ident_bf")
+        nc.vector.tensor_copy(out=ident_bf[:], in_=ident[:])
+        warm = one.tile([P, 1], F32, name="warm")
+        nc.vector.memset(warm[:], 1.0)
+        warm_out = one.tile([P, 1], F32, name="warm_out")
+        nc.scalar.activation(out=warm_out[:], in_=warm[:], func=ACT.Sign)
+        norm_row = one.tile([P, M], BF16, name="norm_row")
+        nc.gpsimd.memset(norm_row[:].bitcast(I32), 0)
+        ones = one.tile([P, P], BF16, name="ones")
+        nc.gpsimd.memset(ones[:], 1.0)
+        dec_s = one.tile([P, 4, D], U8, name="dec_s", align_bytes=64)
+        nc.gpsimd.memset(dec_s[:].bitcast(I32), 0)
+
+        x_col = one.tile([P, 8], F32, name="x_col")
+        bias = one.tile([P, 16], BF16, name="bias")
+        norm_r = one.tile([P, 8], BF16, name="norm_r")
+        norm_c = one.tile([P, 8], BF16, name="norm_c")
+        dec_w = one.tile([P, 4, 2 * D], U8, name="dec_w", align_bytes=64)
+        xb, w_raw, c_raw = {}, {}, {}
+
+        x_rows = x_bytes.rearrange("(q r u) d -> q r (u d)", r=P, u=2)
+        w_rows = w_enc.rearrange("(g p j) f -> g p j f", p=P, j=4)
+        c_rows = concepts.rearrange("(g p e u) c -> g u p e c", p=P, e=2, u=2)
+
+        def load_x(q):
+            xb[q] = one.tile([P, 2 * D], U8, name="xb%d" % q, align_bytes=64)
+            nc.sync.dma_start(out=xb[q][:], in_=x_rows[q])
+
+        def load_w(gf, g):
+            w_raw[gf, g] = roll.tile([P, 4, 512], BF16, tag="w_raw", bufs=6, name="w_raw")
+            nc.sync.dma_start(out=w_raw[gf, g][:], in_=w_rows[g][:, :, 512 * gf : 512 * gf + 512])
+
+        def load_c(g):
+            c_raw[g] = one.tile([P, 4, C], BF16, name="c_raw%d" % g)
+            for u in range(2):
+                nc.sync.dma_start(out=c_raw[g][:, 2 * u : 2 * u + 2, :], in_=c_rows[g, u])
+
+        nc.sync.dma_start(
+            out=x_col[:].rearrange("p (g t) -> p g t", t=4),
+            in_=x_scale.rearrange("o (g p t) -> p (o g) t", p=P, t=4),
+        )
+        load_x(0)
+        load_w(0, 0)
+        load_x(1)
+        load_w(0, 1)
+        nc.sync.dma_start(
+            out=bias[:].rearrange("p (g t) -> p g t", t=4), in_=b.rearrange("(g p t) -> p g t", p=P, t=4)
+        )
+        nc.sync.dma_start(out=norm_row[0:1, :], in_=norms.unsqueeze(0))
+        nc.sync.dma_start(
+            out=norm_c[:].rearrange("p (g j) -> p g j", j=4), in_=norms.rearrange("(g p j) -> p g j", p=P, j=4)
+        )
+        nc.sync.dma_start(
+            out=norm_r[:].rearrange("r (q u) -> r q u", u=2), in_=norms.rearrange("(q r u) -> r q u", r=P, u=2)
+        )
+        load_x(2)
+        load_x(3)
+        load_w(1, 0)
+        load_w(1, 1)
+        load_w(2, 0)
+        load_w(2, 1)
+        load_c(0)
+        load_c(1)
+        load_w(3, 0)
+        load_w(3, 1)
+        nc.sync.dma_start(out=dec_w[:], in_=dec_words.rearrange("g p n -> p g n"))
+        ds = dec_scales.bitcast(I32).rearrange("g q n -> q g n")
+        for quad in range(4):
+            nc.sync.dma_start(
+                out=dec_s[32 * quad : 32 * quad + 4].bitcast(I32), in_=ds[4 * quad : 4 * quad + 4]
+            )
+
+        def spread(dst, src, engs):
+            n = dst.shape[1] // len(engs)
+            for k in range(len(engs)):
+                part = slice(n * k, n * k + n)
+                if engs[k] == "S":
+                    nc.scalar.copy(out=dst[:, part], in_=src[:, part])
+                elif engs[k] == "V":
+                    nc.vector.tensor_copy(out=dst[:, part], in_=src[:, part])
+                else:
+                    nc.gpsimd.tensor_scalar(
+                        out=dst[:, part], in0=src[:, part], scalar1=1.0, scalar2=0.0, op0=ALU.mult, op1=ALU.add
+                    )
+
+        x_codes = [one.tile([P, 2, 512], U32, name="x_codes%d" % G, align_bytes=64) for G in range(2)]
+        x_scales = [one.tile([P, 2, 512], U8, name="x_scales%d" % G, align_bytes=64) for G in range(2)]
+        x_grp = [one.tile([P, 2, 512, 4], BF16, name="x_grp%d" % G, align_bytes=64) for G in range(2)]
+        x_wide, x_turn = {}, {}
+
+        def x_cols(i):
+            return i // 4, 256 * (i % 2) + 128 * (i // 2 % 2)
+
+        def widen(i, eng):
+            x_wide[i] = roll.tile([P, D], BF16, tag="x_wide", bufs=3, name="x_wide")
+            src = xb[i // 2][:, D * (i % 2) : D * (i % 2) + D].bitcast(FP8)
+            if eng == "S":
+                nc.scalar.copy(out=x_wide[i][:], in_=src)
+            else:
+                nc.vector.tensor_copy(out=x_wide[i][:], in_=src)
+
+        def x_transpose(i):
+            x_turn[i] = psum.tile([P, 4, P], F32, tag="tr", bufs=T_BANKS, name="tr")
+            words = x_wide[i][:].bitcast(F32)
+            for g in range(2):
+                for u in range(2):
+                    nc.tensor.transpose(
+                        x_turn[i][:, 2 * g + u, :], words[:, 256 * g + u : 256 * g + 256 : 2], ident[:]
+                    )
+
+        def x_scale_mul(i):
+            G, c0 = x_cols(i)
+            turned = x_turn[i][:].bitcast(BF16)
+            for g in range(2):
+                nc.vector.tensor_tensor(
+                    out=x_grp[G][:, g, c0 : c0 + P, :].rearrange("p r (u e) -> p r u e", u=2),
+                    in0=turned[:, 2 * g : 2 * g + 2, :].rearrange("p u (r e) -> p r u e", e=2),
+                    in1=x_col[:, 4 * g : 4 * g + 4]
+                    .rearrange("p (u e) -> p u e", u=2)
+                    .unsqueeze(1)
+                    .to_broadcast([P, P, 2, 2]),
+                    op=ALU.mult,
+                )
+
+        def x_quant(i):
+            G, c0 = x_cols(i)
+            for g in range(2):
+                nc.vector.quantize_mx(
+                    out=x_codes[G][:, g, c0 : c0 + P].bitcast(FP8X4),
+                    scales=x_scales[G][:, g, c0 : c0 + P],
+                    in_=x_grp[G][:, g, c0 : c0 + P, :].rearrange("p r t -> p (r t)"),
+                )
+
+        w_codes = [one.tile([P, 2, 512], U32, name="w_codes%d" % f, align_bytes=64) for f in range(4)]
+        w_scales = [one.tile([P, 2, 512], U8, name="w_scales%d" % f, align_bytes=64) for f in range(4)]
+        w_grp = {}
+
+        def w_interleave(gf, g, eng):
+            w_grp[gf, g] = roll.tile([P, 4, P, 4], BF16, tag="w_grp", bufs=3, name="w_grp", align_bytes=64)
+            if eng[0] == "P":
+                pe_interleave(
+                    w_raw[gf, g][:].rearrange("p j (m t) -> p t m j", t=4),
+                    w_grp[gf, g][:].rearrange("p t m j -> p (t m j)"),
+                    eng[1:],
+                )
+                return
+            dst = w_grp[gf, g][:]
+            src = w_raw[gf, g][:].rearrange("p j (m t) -> p t m j", t=4)
+            spread(dst, src, eng)
+
+        def pe_interleave(src, dst, engs):
+            banks = []
+            for h in range(2):
+                bank = psum.tile([P, 1024], BF16, tag="tr", bufs=T_BANKS, name="tr")
+                for k in range(2):
+                    nc.tensor.matmul(
+                        bank[:, 512 * k : 512 * k + 512].rearrange("p (m j) -> p m j", j=4),
+                        lhsT=ident_bf[:],
+                        rhs=src[:, 2 * h + k],
+                        start=True,
+                        stop=True,
+                    )
+                banks.append(bank)
+            for h in range(2):
+                part = dst[:, 1024 * h : 1024 * h + 1024]
+                if engs[h] == "S":
+                    nc.scalar.copy(out=part, in_=banks[h][:])
+                else:
+                    nc.vector.tensor_copy(out=part, in_=banks[h][:])
+
+        def w_quant(gf, g):
+            nc.vector.quantize_mx(
+                out=w_codes[gf][:, g, :].bitcast(FP8X4),
+                scales=w_scales[gf][:, g, :],
+                in_=w_grp[gf, g][:].rearrange("p t m j -> p (t m j)"),
+            )
+
+        norm_abs = one.tile([P, M], BF16, name="norm_abs")
+        sign_c = one.tile([P, 8], F32, name="sign_c")
+        sign_r = one.tile([P, 8], F32, name="sign_r")
+
+        def spread_norms():
+            nc.scalar.activation(out=sign_c[:], in_=norm_c[:], func=ACT.Sign)
+            nc.scalar.activation(out=sign_r[:], in_=norm_r[:], func=ACT.Sign)
+            for G in range(2):
+                row = psum.tile([P, 4, P], F32, tag="tr", bufs=T_BANKS, name="tr")
+                flat = row[:].rearrange("p a c -> p (a c)")
+                nc.tensor.matmul(flat, lhsT=ones[:], rhs=norm_row[:, 512 * G : 512 * G + 512], start=True, stop=True)
+                nc.scalar.activation(
+                    out=norm_abs[:, 512 * G : 512 * G + 512].rearrange("p (u h r) -> p u h r", u=2, h=2),
+                    in_=flat.rearrange("p (h r u) -> p u h r", h=2, u=2),
+                    func=ACT.Abs,
+                )
+
+        c_codes = one.tile([P, 2, C], U32, name="c_codes", align_bytes=64)
+        c_scales = one.tile([P, 2, C], U8, name="c_scales", align_bytes=64)
+        c_grp = {}
+
+        def c_sign(g):
+            for t in range(4):
+                j = 4 * g + 2 * (t % 2) + t // 2
+                nc.gpsimd.tensor_scalar(
+                    out=c_raw[g][:, t, :],
+                    in0=c_raw[g][:, t, :],
+                    scalar1=sign_c[:, j : j + 1],
+                    scalar2=0.0,
+                    op0=ALU.mult,
+                    op1=ALU.add,
+                )
+
+        def c_interleave(g, eng):
+            c_grp[g] = roll.tile([P, C, 4], BF16, tag="c_grp", bufs=2, name="c_grp", align_bytes=64)
+            if eng[0] == "P":
+                pe_interleave(
+                    c_raw[g][:].rearrange("p t (b c) -> p b c t", b=4),
+                    c_grp[g][:].rearrange("p c t -> p (c t)"),
+                    eng[1:],
+                )
+                return
+            dst = c_grp[g][:].rearrange("p (c i) t -> p c t i", i=4)
+            src = c_raw[g][:].rearrange("p t (c i) -> p c t i", i=4)
+            spread(dst, src, eng)
+
+        def c_quant(g):
+            nc.vector.quantize_mx(
+                out=c_codes[:, g, :].bitcast(FP8X4),
+                scales=c_scales[:, g, :],
+                in_=c_grp[g][:].rearrange("p c t -> p (c t)"),
+            )
+
+        z_ps, y, b_turn, a_grp, b_grp = {}, {}, {}, {}, {}
+        a_codes, a_scales = {}, {}
+        b_codes = [one.tile([P, 2, 512], U32, name="b_codes%d" % f, align_bytes=64) for f in range(4)]
+        b_scales = [one.tile([P, 2, 512], U8, name="b_scales%d" % f, align_bytes=64) for f in range(4)]
+
+        def encode(gf, G, t):
+            z = psum.tile([P, 512], F32, tag="z", bufs=Z_BANKS, name="z")
+            z_ps[gf, G, t] = z
+            for g in range(2):
+                nc.tensor.matmul_mx(
+                    out=z[:],
+                    lhsT=w_codes[gf][:, g, P * t : P * t + P].bitcast(FP8X4),
+                    lhsT_scale=w_scales[gf][:, g, P * t : P * t + P],
+                    rhs=x_codes[G][:, g, :].bitcast(FP8X4),
+                    rhs_scale=x_scales[G][:, g, :],
+                    start=(g == 0),
+                    stop=(g == 1),
+                )
+
+        def drain(gf, G, t):
+            if t == 0:
+                y[gf, G] = roll.tile([P, 4, 512], BF16, tag="y", bufs=3, name="y")
+            nc.vector.scalar_tensor_tensor(
+                out=y[gf, G][:, t, :],
+                in0=z_ps[gf, G, t][:],
+                scalar=bias[:, 4 * gf + t : 4 * gf + t + 1],
+                in1=norm_abs[:, 512 * G : 512 * G + 512],
+                op0=ALU.add,
+                op1=ALU.mult,
+            )
+
+        def relu(gf, G, h):
+            half = y[gf, G][:, 2 * h : 2 * h + 2, :]
+            nc.vector.tensor_scalar_max(out=half, in0=half, scalar1=0.0)
+
+        def turn(gf, G, h):
+            bank = psum.tile([P, 4, P], F32, tag="tr", bufs=T_BANKS, name="tr")
+            b_turn[gf, G, h] = bank
+            for t in range(2):
+                words = y[gf, G][:, 2 * h + t, :].bitcast(F32)
+                for u in range(2):
+                    nc.tensor.transpose(bank[:, 2 * t + u, :], words[:, P * u : P * u + P], ident[:])
+
+        def turn_out(gf, G, h, eng):
+            if h == 0:
+                b_grp[gf, G] = roll.tile([P, 2048], BF16, tag="b_grp", bufs=2, name="b_grp", align_bytes=64)
+            dst = b_grp[gf, G][:, 1024 * h : 1024 * h + 1024].bitcast(F32)
+            dst = dst.rearrange("p (t m u) -> p t m u", t=2, u=2)
+            src = b_turn[gf, G, h][:].rearrange("p (t u) m -> p t m u", t=2)
+            if eng == "S":
+                nc.scalar.copy(out=dst, in_=src)
+            else:
+                nc.vector.tensor_copy(out=dst, in_=src)
+
+        def quant_b(gf, G):
+            nc.vector.quantize_mx(
+                out=b_codes[gf][:, G, :].bitcast(FP8X4), scales=b_scales[gf][:, G, :], in_=b_grp[gf, G][:]
+            )
+
+        def interleave_a(gf, G, eng):
+            a_grp[gf, G] = roll.tile([P, 512, 4], BF16, tag="a_grp", bufs=2, name="a_grp", align_bytes=64)
+            if eng[0] == "P":
+                pe_interleave(
+                    y[gf, G][:].rearrange("p t (b c) -> p b c t", b=4),
+                    a_grp[gf, G][:].rearrange("p c t -> p (c t)"),
+                    eng[1:],
+                )
+                return
+            dst = a_grp[gf, G][:].rearrange("p (c i) t -> p c t i", i=4)
+            src = y[gf, G][:].rearrange("p t (c i) -> p c t i", i=4)
+            spread(dst, src, eng)
+
+        def quant_a(gf, G):
+            a_codes[gf, G] = one.tile([P, 512], U32, name="a_codes%d%d" % (gf, G), align_bytes=64)
+            a_scales[gf, G] = one.tile([P, 512], U8, name="a_scales%d%d" % (gf, G), align_bytes=64)
+            nc.vector.quantize_mx(
+                out=a_codes[gf, G][:].bitcast(FP8X4),
+                scales=a_scales[gf, G][:],
+                in_=a_grp[gf, G][:].rearrange("p c t -> p (c t)"),
+            )
+
+        o_ps, o_sb = {}, {}
+        recon_rows = out_0.rearrange("(q r u) d -> q u r d", r=P, u=2)
+        assoc_rows = out_1.rearrange("(g m s t) c -> g s m t c", m=P, s=2, t=2)
+
+        def assoc(gf, t):
+            acc = psum.tile([P, 512], F32, tag="o", bufs=O_BANKS, name="acc")
+            o_ps["a", gf, t] = acc
+            for G in range(2):
+                nc.tensor.matmul_mx(
+                    out=acc[:],
+                    lhsT=b_codes[gf][:, G, P * t : P * t + P].bitcast(FP8X4),
+                    lhsT_scale=b_scales[gf][:, G, P * t : P * t + P],
+                    rhs=c_codes[:, G, :].bitcast(FP8X4),
+                    rhs_scale=c_scales[:, G, :],
+                    start=(G == 0),
+                    stop=(G == 1),
+                )
+
+        def assoc_out(gf, t, eng):
+            if t % 2 == 0:
+                o_sb["a", gf, t // 2] = roll.tile([P, 2, 512], F32, tag="o_sb", bufs=6, name="o_sb")
+            dst = o_sb["a", gf, t // 2]
+            if eng == "S":
+                nc.scalar.copy(out=dst[:, t % 2, :], in_=o_ps["a", gf, t][:])
+            else:
+                nc.vector.tensor_copy(out=dst[:, t % 2, :], in_=o_ps["a", gf, t][:])
+            if t % 2 == 1:
+                nc.sync.dma_start(out=assoc_rows[gf, t // 2], in_=dst[:])
+
+        def recon(i, n, first=0, last=4, tag="o"):
+            G, c0 = x_cols(i)
+            if first == 0:
+                o_ps["r", i, n] = psum.tile([P, 512], F32, tag=tag, bufs=O_BANKS if tag == "o" else Z_BANKS, name="acc")
+            for gf in range(first, last):
+                nc.tensor.matmul_mx(
+                    out=o_ps["r", i, n][:],
+                    lhsT=a_codes[gf, G][:, c0 : c0 + P].bitcast(FP8X4),
+                    lhsT_scale=a_scales[gf, G][:, c0 : c0 + P],
+                    rhs=dec_w[:, gf, 1024 * n : 1024 * n + 1024].bitcast(FP4X4),
+                    rhs_scale=dec_s[:, gf, 512 * n : 512 * n + 512],
+                    start=(gf == 0),
+                    stop=(gf == 3),
+                )
+
+        def recon_out(i, n, eng):
+            if n == 0:
+                o_sb["r", i] = roll.tile([P, 2, 512], F32, tag="o_sb", bufs=6, name="o_sb")
+            dst = o_sb["r", i]
+            sign = sign_r[:, i : i + 1]
+            if eng == "S":
+                nc.scalar.activation(out=dst[:, n, :], in_=o_ps["r", i, n][:], func=ACT.Copy, scale=sign)
+            else:
+                nc.vector.tensor_scalar_mul(out=dst[:, n, :], in0=o_ps["r", i, n][:], scalar1=sign)
+            if n == 1:
+                nc.sync.dma_start(out=recon_rows[i // 2, i % 2], in_=dst[:].rearrange("p n d -> p (n d)"))
+
+        W_ROADS = (("S","SS"),("V","S"),("S","S"),("S","S"))
+        C_ROADS = ("S","S")
+        A_ROADS = ("S","SS","S","S","S","SS","V","S")
+        HEAD_WIDEN, WIDEN = "VVSV", "S"
+        OUT_ENGINES = "SSSV"
+        FILL_AT = (0,1,1,2,5)
+        FLUSH = (2,0,2,1,1,1,1,1,2,2)
+        units = [(0, 0), (1, 0), (2, 0), (3, 0), (0, 1), (1, 1), (2, 1), (3, 1)]
+        TQ, TB, TE, TI, LAG, TP, EARLY, ASSOC_FIRST = (0,1), (1,1), (1,1), 3, 1, 2, 3, False
+
+        w_interleave(0, 0, W_ROADS[0][0])
+        for i in range(5):
+            if i < 4:
+                widen(i, HEAD_WIDEN[i])
+                x_transpose(i)
+            if i >= 1:
+                x_scale_mul(i - 1)
+            if i >= 2:
+                x_quant(i - 2)
+            if i == 3:
+                w_quant(0, 0)
+        w_interleave(0, 1, W_ROADS[0][1])
+        spread_norms()
+        x_quant(3)
+        w_quant(0, 1)
+        for g in range(2):
+            c_sign(g)
+
+        def w_fill(gf):
+            return [
+                lambda: w_interleave(gf, 0, W_ROADS[gf][0]),
+                lambda: w_interleave(gf, 1, W_ROADS[gf][1]),
+                lambda: w_quant(gf, 0),
+                lambda: w_quant(gf, 1),
+            ]
+
+        def x_fill():
+            steps = []
+            for i in range(4, 9):
+                if i < 8:
+                    steps.append(lambda i=i: widen(i, WIDEN))
+                    if i == 4:
+                        steps.append(lambda i=i: x_transpose(i))
+                    else:
+                        steps.append(lambda i=i: x_quant(i - 2) if i > 5 else None)
+                if i >= 5:
+                    steps.append(lambda i=i: x_scale_mul(i - 1))
+                    if i < 8:
+                        steps.append(lambda i=i: x_transpose(i))
+            steps.append(lambda: x_quant(6))
+            steps.append(lambda: x_quant(7))
+            return steps
+
+        c_fill = [
+            lambda: c_interleave(0, C_ROADS[0]),
+            lambda: c_interleave(1, C_ROADS[1]),
+            lambda: c_quant(0),
+            lambda: c_quant(1),
+        ]
+        fills = {}
+        for at, steps in zip(FILL_AT, (w_fill(1), x_fill(), w_fill(2), w_fill(3), c_fill)):
+            fills.setdefault(at, []).extend(steps)
+        c_step = FILL_AT[4]
+
+        waiting, opened, early, done_a, done_b, turn_no = [], [], [], [], [], [0]
+
+        def empty_one(eng=None):
+            kind, i, n = opened.pop(0)
+            if eng is None:
+                eng = OUT_ENGINES[turn_no[0] % len(OUT_ENGINES)]
+                turn_no[0] += 1
+            if kind == "a":
+                assoc_out(i, n, eng)
+            else:
+                recon_out(i, n, eng)
+
+        def flush(count):
+            for step in range(count):
+                if waiting:
+                    kind, i, n = waiting.pop(0)
+                    if kind == "a":
+                        assoc(i, n)
+                    else:
+                        recon(i, n)
+                    opened.append((kind, i, n))
+                    while len(opened) > LAG:
+                        empty_one()
+
+        def after_b(gf, G):
+            done_b.append((gf, G))
+            if (gf, 1 - G) in done_b:
+                jobs = [("a", gf, t) for t in range(4)]
+                if ASSOC_FIRST:
+                    waiting[0:0] = jobs
+                else:
+                    waiting.extend(jobs)
+
+        def after_a(gf, G):
+            done_a.append((gf, G))
+            if len([1 for f in range(4) if (f, G) in done_a]) == 4:
+                waiting.extend([("r", 4 * G + j, n) for j in range(4) for n in range(2) if (4 * G + j, n) not in early])
+
+        for s in range(10):
+            now = units[s] if s < 8 else None
+            prev = units[s - 1] if 1 <= s <= 8 else None
+            old = units[s - 2] if s >= 2 else None
+            fill = fills.get(s, [])
+            for t in range(4):
+                if now:
+                    encode(now[0], now[1], t)
+                if old and t == TQ[0]:
+                    quant_b(*old)
+                    after_b(*old)
+                if old and t == TQ[1]:
+                    quant_a(*old)
+                    after_a(*old)
+                if prev and t == 0:
+                    relu(prev[0], prev[1], 1)
+                for h in range(2):
+                    if prev and t == TB[h]:
+                        turn(prev[0], prev[1], h)
+                for h in range(2):
+                    if prev and t == TE[h]:
+                        turn_out(prev[0], prev[1], h, "S")
+                if prev and t == TI:
+                    interleave_a(prev[0], prev[1], A_ROADS[s - 1])
+                for k in range(t * len(fill) // 4, (t + 1) * len(fill) // 4):
+                    fill[k]()
+                if now:
+                    drain(now[0], now[1], t)
+                if now and t == 2:
+                    relu(now[0], now[1], 0)
+                if s == 8 and t == TP:
+                    flush(100)
+                    for k in range(EARLY):
+                        early.append((4 * units[7][1] + k // 2, k % 2))
+                        recon(early[k][0], early[k][1], 0, 3, "z")
+                if s == 9 and t == TQ[1]:
+                    for i, n in early:
+                        recon(i, n, 3, 4)
+                        recon_out(i, n, "SV"[turn_no[0] % 2])
+                        turn_no[0] += 1
+                if not (s == 8 and t >= TP):
+                    flush(FLUSH[s] if now else 4)
+        flush(100)
+        for k in range(len(opened)):
+            empty_one("SV"[k % 2])

@@ -37,17 +37,14 @@ def tile_sae_decode_concepts_s8_kernel(
         nc.vector.memset(warm[:], 1.0)
         warm_out = one.tile([P, 1], F32, name="warm_out")
         nc.scalar.activation(out=warm_out[:], in_=warm[:], func=ACT.Sign)
-        norm_row = one.tile([P, M], BF16, name="norm_row")
-        nc.gpsimd.memset(norm_row[:].bitcast(I32), 0)
+        rows = one.tile([P, F + M], BF16, name="rows")
+        nc.vector.memset(rows[:].bitcast(I32), 0)
         ones = one.tile([P, P], BF16, name="ones")
         nc.gpsimd.memset(ones[:], 1.0)
         dec_s = one.tile([P, 4, D], U8, name="dec_s", align_bytes=64)
         nc.gpsimd.memset(dec_s[:].bitcast(I32), 0)
 
         x_col = one.tile([P, 8], F32, name="x_col")
-        bias = one.tile([P, 16], BF16, name="bias")
-        norm_r = one.tile([P, 8], BF16, name="norm_r")
-        norm_c = one.tile([P, 8], BF16, name="norm_c")
         dec_w = one.tile([P, 4, 2 * D], U8, name="dec_w", align_bytes=64)
         xb, w_raw, c_raw = {}, {}, {}
 
@@ -76,16 +73,8 @@ def tile_sae_decode_concepts_s8_kernel(
         load_w(0, 0)
         load_x(1)
         load_w(0, 1)
-        nc.sync.dma_start(
-            out=bias[:].rearrange("p (g t) -> p g t", t=4), in_=b.rearrange("(g p t) -> p g t", p=P, t=4)
-        )
-        nc.sync.dma_start(out=norm_row[0:1, :], in_=norms.unsqueeze(0))
-        nc.sync.dma_start(
-            out=norm_c[:].rearrange("p (g j) -> p g j", j=4), in_=norms.rearrange("(g p j) -> p g j", p=P, j=4)
-        )
-        nc.sync.dma_start(
-            out=norm_r[:].rearrange("r (q u) -> r q u", u=2), in_=norms.rearrange("(q r u) -> r q u", r=P, u=2)
-        )
+        nc.sync.dma_start(out=rows[0:1, :F], in_=b.unsqueeze(0))
+        nc.sync.dma_start(out=rows[0:1, F:], in_=norms.unsqueeze(0))
         load_x(2)
         load_x(3)
         load_w(1, 0)
@@ -209,21 +198,33 @@ def tile_sae_decode_concepts_s8_kernel(
             )
 
         norm_abs = one.tile([P, M], BF16, name="norm_abs")
-        sign_c = one.tile([P, 8], F32, name="sign_c")
-        sign_r = one.tile([P, 8], F32, name="sign_r")
+        bias = one.tile([P, 16], F32, name="bias")
+        signs = one.tile([P, 16], F32, name="signs")
+        sign_c, sign_r = signs[:, 0:8], signs[:, 8:16]
 
         def spread_norms():
-            nc.scalar.activation(out=sign_c[:], in_=norm_c[:], func=ACT.Sign)
-            nc.scalar.activation(out=sign_r[:], in_=norm_r[:], func=ACT.Sign)
             for G in range(2):
-                row = psum.tile([P, 4, P], F32, tag="tr", bufs=T_BANKS, name="tr")
-                flat = row[:].rearrange("p a c -> p (a c)")
-                nc.tensor.matmul(flat, lhsT=ones[:], rhs=norm_row[:, 512 * G : 512 * G + 512], start=True, stop=True)
+                row = psum.tile([P, 512], F32, tag="tr", bufs=T_BANKS, name="tr")
+                nc.tensor.matmul(
+                    row[:], lhsT=ones[:], rhs=rows[:, F + 512 * G : F + 512 * G + 512], start=True, stop=True
+                )
                 nc.scalar.activation(
                     out=norm_abs[:, 512 * G : 512 * G + 512].rearrange("p (u h r) -> p u h r", u=2, h=2),
-                    in_=flat.rearrange("p (h r u) -> p u h r", h=2, u=2),
+                    in_=row[:].rearrange("p (h r u) -> p u h r", h=2, u=2),
                     func=ACT.Abs,
                 )
+
+        def spread_columns():
+            cols = psum.tile([P, 32], F32, tag="tr", bufs=T_BANKS, name="tr")
+            picks = [(512 * g + t, 512 * g + 512, 4) for g in range(4) for t in range(4)]
+            picks += [(F + 512 * g + j, F + 512 * g + 512, 4) for g in range(2) for j in range(4)]
+            picks += [(F + 256 * q + u, F + 256 * q + 256, 2) for q in range(4) for u in range(2)]
+            for k, (lo, hi, step) in enumerate(picks):
+                nc.tensor.matmul(
+                    cols[:, k : k + 1], lhsT=rows[:, lo:hi:step], rhs=ones[:, 0:1], start=True, stop=True
+                )
+            nc.vector.tensor_copy(out=bias[:], in_=cols[:, 0:16])
+            nc.scalar.activation(out=signs[:], in_=cols[:, 16:32], func=ACT.Sign)
 
         c_codes = one.tile([P, 2, C], U32, name="c_codes", align_bytes=64)
         c_scales = one.tile([P, 2, C], U8, name="c_scales", align_bytes=64)
@@ -232,13 +233,8 @@ def tile_sae_decode_concepts_s8_kernel(
         def c_sign(g):
             for t in range(4):
                 j = 4 * g + 2 * (t % 2) + t // 2
-                nc.gpsimd.tensor_scalar(
-                    out=c_raw[g][:, t, :],
-                    in0=c_raw[g][:, t, :],
-                    scalar1=sign_c[:, j : j + 1],
-                    scalar2=0.0,
-                    op0=ALU.mult,
-                    op1=ALU.add,
+                nc.vector.tensor_scalar_mul(
+                    out=c_raw[g][:, t, :], in0=c_raw[g][:, t, :], scalar1=sign_c[:, j : j + 1]
                 )
 
         def c_interleave(g, eng):
@@ -250,8 +246,8 @@ def tile_sae_decode_concepts_s8_kernel(
                     eng[1:],
                 )
                 return
-            dst = c_grp[g][:].rearrange("p (c i) t -> p c t i", i=4)
-            src = c_raw[g][:].rearrange("p t (c i) -> p c t i", i=4)
+            dst = c_grp[g][:]
+            src = c_raw[g][:].rearrange("p t c -> p c t")
             spread(dst, src, eng)
 
         def c_quant(g):
@@ -329,8 +325,8 @@ def tile_sae_decode_concepts_s8_kernel(
                     eng[1:],
                 )
                 return
-            dst = a_grp[gf, G][:].rearrange("p (c i) t -> p c t i", i=4)
-            src = y[gf, G][:].rearrange("p t (c i) -> p c t i", i=4)
+            dst = a_grp[gf, G][:]
+            src = y[gf, G][:].rearrange("p t c -> p c t")
             spread(dst, src, eng)
 
         def quant_a(gf, G):
@@ -420,11 +416,10 @@ def tile_sae_decode_concepts_s8_kernel(
             if i == 3:
                 w_quant(0, 0)
         w_interleave(0, 1, W_ROADS[0][1])
+        spread_columns()
         spread_norms()
         x_quant(3)
         w_quant(0, 1)
-        for g in range(2):
-            c_sign(g)
 
         def w_fill(gf):
             return [
@@ -452,6 +447,8 @@ def tile_sae_decode_concepts_s8_kernel(
             return steps
 
         c_fill = [
+            lambda: c_sign(0),
+            lambda: c_sign(1),
             lambda: c_interleave(0, C_ROADS[0]),
             lambda: c_interleave(1, C_ROADS[1]),
             lambda: c_quant(0),

from contextlib import ExitStack

import concourse.mybir as mybir
from concourse.masks import make_identity

F32 = mybir.dt.float32
BF16 = mybir.dt.bfloat16
I32 = mybir.dt.int32
U32 = mybir.dt.uint32
U8 = mybir.dt.uint8
FP8 = mybir.dt.float8_e4m3fn
FP8X4 = mybir.dt.float8_e4m3fn_x4
FP4X4 = mybir.dt.float4_e2m1fn_x4
ALU = mybir.AluOpType
ACT = mybir.ActivationFunctionType

M, D, F, C = 1024, 1024, 2048, 512
P = 128
Z_BANKS, T_BANKS, O_BANKS = 3, 2, 3
FLOPS = 2 * (2 * M * D * F + F * M * C)


def tile_sae_decode_concepts_s8_kernel(
    tc, x_bytes, x_scale, w_enc, b, norms, dec_words, dec_scales, concepts, out_0, out_1
):
    nc = tc.nc
    with ExitStack() as ctx:
        one = ctx.enter_context(tc.tile_pool(name="one", bufs=1))
        roll = ctx.enter_context(tc.tile_pool(name="roll", bufs=2))
        psum = ctx.enter_context(tc.psum_pool(name="psum", bufs=2))

        ident = one.tile([P, P], F32, name="ident")
        make_identity(nc, ident[:])
        ident_bf = one.tile([P, P], BF16, name="ident_bf")
        nc.vector.tensor_copy(out=ident_bf[:], in_=ident[:])
        warm = one.tile([P, 1], F32, name="warm")
        nc.vector.memset(warm[:], 1.0)
        warm_out = one.tile([P, 1], F32, name="warm_out")
        nc.scalar.activation(out=warm_out[:], in_=warm[:], func=ACT.Sign)
        rows = one.tile([P, F + M], BF16, name="rows")
        nc.vector.memset(rows[:].bitcast(I32), 0)
        ones = one.tile([P, P], BF16, name="ones")
        nc.gpsimd.memset(ones[:], 1.0)
        dec_s = one.tile([P, 4, D], U8, name="dec_s", align_bytes=64)
        nc.gpsimd.memset(dec_s[:].bitcast(I32), 0)

        x_col = one.tile([P, 8], F32, name="x_col")
        dec_w = one.tile([P, 4, 2 * D], U8, name="dec_w", align_bytes=64)
        xb, w_raw, c_raw = {}, {}, {}

        x_rows = x_bytes.rearrange("(q r u) d -> q r (u d)", r=P, u=2)
        w_rows = w_enc.rearrange("(g p j) f -> g p j f", p=P, j=4)
        c_rows = concepts.rearrange("(g p e u) c -> g u p e c", p=P, e=2, u=2)

        def load_x(q):
            xb[q] = one.tile([P, 2 * D], U8, name="xb%d" % q, align_bytes=64)
            nc.sync.dma_start(out=xb[q][:], in_=x_rows[q])

        def load_w(gf, g):
            w_raw[gf, g] = roll.tile([P, 4, 512], BF16, tag="w_raw", bufs=6, name="w_raw")
            nc.sync.dma_start(out=w_raw[gf, g][:], in_=w_rows[g][:, :, 512 * gf : 512 * gf + 512])

        def load_c(g):
            c_raw[g] = one.tile([P, 4, C], BF16, name="c_raw%d" % g)
            for u in range(2):
                nc.sync.dma_start(out=c_raw[g][:, 2 * u : 2 * u + 2, :], in_=c_rows[g, u])

        nc.sync.dma_start(
            out=x_col[:].rearrange("p (g t) -> p g t", t=4),
            in_=x_scale.rearrange("o (g p t) -> p (o g) t", p=P, t=4),
        )
        load_x(0)
        load_w(0, 0)
        load_x(1)
        load_w(0, 1)
        nc.sync.dma_start(out=rows[0:1, :F], in_=b.unsqueeze(0))
        nc.sync.dma_start(out=rows[0:1, F:], in_=norms.unsqueeze(0))
        load_x(2)
        load_x(3)
        load_w(1, 0)
        load_w(1, 1)
        load_w(2, 0)
        load_w(2, 1)
        load_c(0)
        load_c(1)
        load_w(3, 0)
        load_w(3, 1)
        nc.sync.dma_start(out=dec_w[:], in_=dec_words.rearrange("g p n -> p g n"))
        ds = dec_scales.bitcast(I32).rearrange("g q n -> q g n")
        for quad in range(4):
            nc.sync.dma_start(
                out=dec_s[32 * quad : 32 * quad + 4].bitcast(I32), in_=ds[4 * quad : 4 * quad + 4]
            )

        def spread(dst, src, engs):
            n = dst.shape[1] // len(engs)
            for k in range(len(engs)):
                part = slice(n * k, n * k + n)
                if engs[k] == "S":
                    nc.scalar.copy(out=dst[:, part], in_=src[:, part])
                elif engs[k] == "V":
                    nc.vector.tensor_copy(out=dst[:, part], in_=src[:, part])
                else:
                    nc.gpsimd.tensor_scalar(
                        out=dst[:, part], in0=src[:, part], scalar1=1.0, scalar2=0.0, op0=ALU.mult, op1=ALU.add
                    )

        x_codes = [one.tile([P, 2, 512], U32, name="x_codes%d" % G, align_bytes=64) for G in range(2)]
        x_scales = [one.tile([P, 2, 512], U8, name="x_scales%d" % G, align_bytes=64) for G in range(2)]
        x_grp = [one.tile([P, 2, 512, 4], BF16, name="x_grp%d" % G, align_bytes=64) for G in range(2)]
        x_wide, x_turn = {}, {}

        def x_cols(i):
            return i // 4, 256 * (i % 2) + 128 * (i // 2 % 2)

        def widen(i, eng):
            x_wide[i] = roll.tile([P, D], BF16, tag="x_wide", bufs=3, name="x_wide")
            src = xb[i // 2][:, D * (i % 2) : D * (i % 2) + D].bitcast(FP8)
            if eng == "S":
                nc.scalar.copy(out=x_wide[i][:], in_=src)
            else:
                nc.vector.tensor_copy(out=x_wide[i][:], in_=src)

        def x_transpose(i):
            x_turn[i] = psum.tile([P, 4, P], F32, tag="tr", bufs=T_BANKS, name="tr")
            words = x_wide[i][:].bitcast(F32)
            for g in range(2):
                for u in range(2):
                    nc.tensor.transpose(
                        x_turn[i][:, 2 * g + u, :], words[:, 256 * g + u : 256 * g + 256 : 2], ident[:]
                    )

        def x_scale_mul(i):
            G, c0 = x_cols(i)
            turned = x_turn[i][:].bitcast(BF16)
            for g in range(2):
                nc.vector.tensor_tensor(
                    out=x_grp[G][:, g, c0 : c0 + P, :].rearrange("p r (u e) -> p r u e", u=2),
                    in0=turned[:, 2 * g : 2 * g + 2, :].rearrange("p u (r e) -> p r u e", e=2),
                    in1=x_col[:, 4 * g : 4 * g + 4]
                    .rearrange("p (u e) -> p u e", u=2)
                    .unsqueeze(1)
                    .to_broadcast([P, P, 2, 2]),
                    op=ALU.mult,
                )

        def x_quant(i):
            G, c0 = x_cols(i)
            for g in range(2):
                nc.vector.quantize_mx(
                    out=x_codes[G][:, g, c0 : c0 + P].bitcast(FP8X4),
                    scales=x_scales[G][:, g, c0 : c0 + P],
                    in_=x_grp[G][:, g, c0 : c0 + P, :].rearrange("p r t -> p (r t)"),
                )

        w_codes = [one.tile([P, 2, 512], U32, name="w_codes%d" % f, align_bytes=64) for f in range(4)]
        w_scales = [one.tile([P, 2, 512], U8, name="w_scales%d" % f, align_bytes=64) for f in range(4)]
        w_grp = {}

        def w_interleave(gf, g, eng):
            w_grp[gf, g] = roll.tile([P, 4, P, 4], BF16, tag="w_grp", bufs=3, name="w_grp", align_bytes=64)
            if eng[0] == "P":
                pe_interleave(
                    w_raw[gf, g][:].rearrange("p j (m t) -> p t m j", t=4),
                    w_grp[gf, g][:].rearrange("p t m j -> p (t m j)"),
                    eng[1:],
                )
                return
            dst = w_grp[gf, g][:]
            src = w_raw[gf, g][:].rearrange("p j (m t) -> p t m j", t=4)
            spread(dst, src, eng)

        def pe_interleave(src, dst, engs):
            banks = []
            for h in range(2):
                bank = psum.tile([P, 1024], BF16, tag="tr", bufs=T_BANKS, name="tr")
                for k in range(2):
                    nc.tensor.matmul(
                        bank[:, 512 * k : 512 * k + 512].rearrange("p (m j) -> p m j", j=4),
                        lhsT=ident_bf[:],
                        rhs=src[:, 2 * h + k],
                        start=True,
                        stop=True,
                    )
                banks.append(bank)
            for h in range(2):
                part = dst[:, 1024 * h : 1024 * h + 1024]
                if engs[h] == "S":
                    nc.scalar.copy(out=part, in_=banks[h][:])
                else:
                    nc.vector.tensor_copy(out=part, in_=banks[h][:])

        def w_quant(gf, g):
            nc.vector.quantize_mx(
                out=w_codes[gf][:, g, :].bitcast(FP8X4),
                scales=w_scales[gf][:, g, :],
                in_=w_grp[gf, g][:].rearrange("p t m j -> p (t m j)"),
            )

        norm_abs = one.tile([P, M], BF16, name="norm_abs")
        bias = one.tile([P, 16], F32, name="bias")
        signs = one.tile([P, 16], F32, name="signs")
        sign_c, sign_r = signs[:, 0:8], signs[:, 8:16]

        def spread_norms():
            for G in range(2):
                row = psum.tile([P, 512], F32, tag="tr", bufs=T_BANKS, name="tr")
                nc.tensor.matmul(
                    row[:], lhsT=ones[:], rhs=rows[:, F + 512 * G : F + 512 * G + 512], start=True, stop=True
                )
                nc.scalar.activation(
                    out=norm_abs[:, 512 * G : 512 * G + 512].rearrange("p (u h r) -> p u h r", u=2, h=2),
                    in_=row[:].rearrange("p (h r u) -> p u h r", h=2, u=2),
                    func=ACT.Abs,
                )

        def spread_columns():
            cols = psum.tile([P, 32], F32, tag="tr", bufs=T_BANKS, name="tr")
            picks = [(512 * g + t, 512 * g + 512, 4) for g in range(4) for t in range(4)]
            picks += [(F + 512 * g + j, F + 512 * g + 512, 4) for g in range(2) for j in range(4)]
            picks += [(F + 256 * q + u, F + 256 * q + 256, 2) for q in range(4) for u in range(2)]
            for k, (lo, hi, step) in enumerate(picks):
                nc.tensor.matmul(
                    cols[:, k : k + 1], lhsT=rows[:, lo:hi:step], rhs=ones[:, 0:1], start=True, stop=True
                )
            nc.vector.tensor_copy(out=bias[:], in_=cols[:, 0:16])
            nc.scalar.activation(out=signs[:], in_=cols[:, 16:32], func=ACT.Sign)

        c_codes = one.tile([P, 2, C], U32, name="c_codes", align_bytes=64)
        c_scales = one.tile([P, 2, C], U8, name="c_scales", align_bytes=64)
        c_grp = {}

        def c_sign(g):
            for t in range(4):
                j = 4 * g + 2 * (t % 2) + t // 2
                nc.vector.tensor_scalar_mul(
                    out=c_raw[g][:, t, :], in0=c_raw[g][:, t, :], scalar1=sign_c[:, j : j + 1]
                )

        def c_interleave(g, eng):
            c_grp[g] = roll.tile([P, C, 4], BF16, tag="c_grp", bufs=2, name="c_grp", align_bytes=64)
            if eng[0] == "P":
                pe_interleave(
                    c_raw[g][:].rearrange("p t (b c) -> p b c t", b=4),
                    c_grp[g][:].rearrange("p c t -> p (c t)"),
                    eng[1:],
                )
                return
            dst = c_grp[g][:]
            src = c_raw[g][:].rearrange("p t c -> p c t")
            spread(dst, src, eng)

        def c_quant(g):
            nc.vector.quantize_mx(
                out=c_codes[:, g, :].bitcast(FP8X4),
                scales=c_scales[:, g, :],
                in_=c_grp[g][:].rearrange("p c t -> p (c t)"),
            )

        z_ps, y, b_turn, a_grp, b_grp = {}, {}, {}, {}, {}
        a_codes, a_scales = {}, {}
        b_codes = [one.tile([P, 2, 512], U32, name="b_codes%d" % f, align_bytes=64) for f in range(4)]
        b_scales = [one.tile([P, 2, 512], U8, name="b_scales%d" % f, align_bytes=64) for f in range(4)]

        def encode(gf, G, t):
            z = psum.tile([P, 512], F32, tag="z", bufs=Z_BANKS, name="z")
            z_ps[gf, G, t] = z
            for g in range(2):
                nc.tensor.matmul_mx(
                    out=z[:],
                    lhsT=w_codes[gf][:, g, P * t : P * t + P].bitcast(FP8X4),
                    lhsT_scale=w_scales[gf][:, g, P * t : P * t + P],
                    rhs=x_codes[G][:, g, :].bitcast(FP8X4),
                    rhs_scale=x_scales[G][:, g, :],
                    start=(g == 0),
                    stop=(g == 1),
                )

        def drain(gf, G, t):
            if t == 0:
                y[gf, G] = roll.tile([P, 4, 512], BF16, tag="y", bufs=3, name="y")
            nc.vector.scalar_tensor_tensor(
                out=y[gf, G][:, t, :],
                in0=z_ps[gf, G, t][:],
                scalar=bias[:, 4 * gf + t : 4 * gf + t + 1],
                in1=norm_abs[:, 512 * G : 512 * G + 512],
                op0=ALU.add,
                op1=ALU.mult,
            )

        def relu(gf, G, h):
            half = y[gf, G][:, 2 * h : 2 * h + 2, :]
            nc.vector.tensor_scalar_max(out=half, in0=half, scalar1=0.0)

        def turn(gf, G, h):
            bank = psum.tile([P, 4, P], F32, tag="tr", bufs=T_BANKS, name="tr")
            b_turn[gf, G, h] = bank
            for t in range(2):
                words = y[gf, G][:, 2 * h + t, :].bitcast(F32)
                for u in range(2):
                    nc.tensor.transpose(bank[:, 2 * t + u, :], words[:, P * u : P * u + P], ident[:])

        def turn_out(gf, G, h, eng):
            if h == 0:
                b_grp[gf, G] = roll.tile([P, 2048], BF16, tag="b_grp", bufs=2, name="b_grp", align_bytes=64)
            dst = b_grp[gf, G][:, 1024 * h : 1024 * h + 1024].bitcast(F32)
            dst = dst.rearrange("p (t m u) -> p t m u", t=2, u=2)
            src = b_turn[gf, G, h][:].rearrange("p (t u) m -> p t m u", t=2)
            if eng == "S":
                nc.scalar.copy(out=dst, in_=src)
            else:
                nc.vector.tensor_copy(out=dst, in_=src)

        def quant_b(gf, G):
            nc.vector.quantize_mx(
                out=b_codes[gf][:, G, :].bitcast(FP8X4), scales=b_scales[gf][:, G, :], in_=b_grp[gf, G][:]
            )

        def interleave_a(gf, G, eng):
            a_grp[gf, G] = roll.tile([P, 512, 4], BF16, tag="a_grp", bufs=2, name="a_grp", align_bytes=64)
            if eng[0] == "P":
                pe_interleave(
                    y[gf, G][:].rearrange("p t (b c) -> p b c t", b=4),
                    a_grp[gf, G][:].rearrange("p c t -> p (c t)"),
                    eng[1:],
                )
                return
            dst = a_grp[gf, G][:]
            src = y[gf, G][:].rearrange("p t c -> p c t")
            spread(dst, src, eng)

        def quant_a(gf, G):
            a_codes[gf, G] = one.tile([P, 512], U32, name="a_codes%d%d" % (gf, G), align_bytes=64)
            a_scales[gf, G] = one.tile([P, 512], U8, name="a_scales%d%d" % (gf, G), align_bytes=64)
            nc.vector.quantize_mx(
                out=a_codes[gf, G][:].bitcast(FP8X4),
                scales=a_scales[gf, G][:],
                in_=a_grp[gf, G][:].rearrange("p c t -> p (c t)"),
            )

        o_ps, o_sb = {}, {}
        recon_rows = out_0.rearrange("(q r u) d -> q u r d", r=P, u=2)
        assoc_rows = out_1.rearrange("(g m s t) c -> g s m t c", m=P, s=2, t=2)

        def assoc(gf, t):
            acc = psum.tile([P, 512], F32, tag="o", bufs=O_BANKS, name="acc")
            o_ps["a", gf, t] = acc
            for G in range(2):
                nc.tensor.matmul_mx(
                    out=acc[:],
                    lhsT=b_codes[gf][:, G, P * t : P * t + P].bitcast(FP8X4),
                    lhsT_scale=b_scales[gf][:, G, P * t : P * t + P],
                    rhs=c_codes[:, G, :].bitcast(FP8X4),
                    rhs_scale=c_scales[:, G, :],
                    start=(G == 0),
                    stop=(G == 1),
                )

        def assoc_out(gf, t, eng):
            if t % 2 == 0:
                o_sb["a", gf, t // 2] = roll.tile([P, 2, 512], F32, tag="o_sb", bufs=6, name="o_sb")
            dst = o_sb["a", gf, t // 2]
            if eng == "S":
                nc.scalar.copy(out=dst[:, t % 2, :], in_=o_ps["a", gf, t][:])
            else:
                nc.vector.tensor_copy(out=dst[:, t % 2, :], in_=o_ps["a", gf, t][:])
            if t % 2 == 1:
                nc.sync.dma_start(out=assoc_rows[gf, t // 2], in_=dst[:])

        def recon(i, n, first=0, last=4, tag="o"):
            G, c0 = x_cols(i)
            if first == 0:
                o_ps["r", i, n] = psum.tile([P, 512], F32, tag=tag, bufs=O_BANKS if tag == "o" else Z_BANKS, name="acc")
            for gf in range(first, last):
                nc.tensor.matmul_mx(
                    out=o_ps["r", i, n][:],
                    lhsT=a_codes[gf, G][:, c0 : c0 + P].bitcast(FP8X4),
                    lhsT_scale=a_scales[gf, G][:, c0 : c0 + P],
                    rhs=dec_w[:, gf, 1024 * n : 1024 * n + 1024].bitcast(FP4X4),
                    rhs_scale=dec_s[:, gf, 512 * n : 512 * n + 512],
                    start=(gf == 0),
                    stop=(gf == 3),
                )

        def recon_out(i, n, eng):
            if n == 0:
                o_sb["r", i] = roll.tile([P, 2, 512], F32, tag="o_sb", bufs=6, name="o_sb")
            dst = o_sb["r", i]
            sign = sign_r[:, i : i + 1]
            if eng == "S":
                nc.scalar.activation(out=dst[:, n, :], in_=o_ps["r", i, n][:], func=ACT.Copy, scale=sign)
            else:
                nc.vector.tensor_scalar_mul(out=dst[:, n, :], in0=o_ps["r", i, n][:], scalar1=sign)
            if n == 1:
                nc.sync.dma_start(out=recon_rows[i // 2, i % 2], in_=dst[:].rearrange("p n d -> p (n d)"))

        W_ROADS = (("S","SS"),("V","S"),("S","S"),("S","S"))
        C_ROADS = ("S","S")
        A_ROADS = ("S","SS","S","S","S","SS","V","S")
        HEAD_WIDEN, WIDEN = "VVSV", "S"
        OUT_ENGINES = "SSSV"
        FILL_AT = (0,1,1,2,5)
        FLUSH = (2,0,2,1,1,1,1,1,2,2)
        units = [(0, 0), (1, 0), (2, 0), (3, 0), (0, 1), (1, 1), (2, 1), (3, 1)]
        TQ, TB, TE, TI, LAG, TP, EARLY, ASSOC_FIRST = (0,1), (1,1), (1,1), 3, 1, 2, 3, False

        w_interleave(0, 0, W_ROADS[0][0])
        for i in range(5):
            if i < 4:
                widen(i, HEAD_WIDEN[i])
                x_transpose(i)
            if i >= 1:
                x_scale_mul(i - 1)
            if i >= 2:
                x_quant(i - 2)
            if i == 3:
                w_quant(0, 0)
        w_interleave(0, 1, W_ROADS[0][1])
        spread_columns()
        spread_norms()
        x_quant(3)
        w_quant(0, 1)

        def w_fill(gf):
            return [
                lambda: w_interleave(gf, 0, W_ROADS[gf][0]),
                lambda: w_interleave(gf, 1, W_ROADS[gf][1]),
                lambda: w_quant(gf, 0),
                lambda: w_quant(gf, 1),
            ]

        def x_fill():
            steps = []
            for i in range(4, 9):
                if i < 8:
                    steps.append(lambda i=i: widen(i, WIDEN))
                    if i == 4:
                        steps.append(lambda i=i: x_transpose(i))
                    else:
                        steps.append(lambda i=i: x_quant(i - 2) if i > 5 else None)
                if i >= 5:
                    steps.append(lambda i=i: x_scale_mul(i - 1))
                    if i < 8:
                        steps.append(lambda i=i: x_transpose(i))
            steps.append(lambda: x_quant(6))
            steps.append(lambda: x_quant(7))
            return steps

        c_fill = [
            lambda: c_sign(0),
            lambda: c_sign(1),
            lambda: c_interleave(0, C_ROADS[0]),
            lambda: c_interleave(1, C_ROADS[1]),
            lambda: c_quant(0),
            lambda: c_quant(1),
        ]
        fills = {}
        for at, steps in zip(FILL_AT, (w_fill(1), x_fill(), w_fill(2), w_fill(3), c_fill)):
            fills.setdefault(at, []).extend(steps)
        c_step = FILL_AT[4]

        waiting, opened, early, done_a, done_b, turn_no = [], [], [], [], [], [0]

        def empty_one(eng=None):
            kind, i, n = opened.pop(0)
            if eng is None:
                eng = OUT_ENGINES[turn_no[0] % len(OUT_ENGINES)]
                turn_no[0] += 1
            if kind == "a":
                assoc_out(i, n, eng)
            else:
                recon_out(i, n, eng)

        def flush(count):
            for step in range(count):
                if waiting:
                    kind, i, n = waiting.pop(0)
                    if kind == "a":
                        assoc(i, n)
                    else:
                        recon(i, n)
                    opened.append((kind, i, n))
                    while len(opened) > LAG:
                        empty_one()

        def after_b(gf, G):
            done_b.append((gf, G))
            if (gf, 1 - G) in done_b:
                jobs = [("a", gf, t) for t in range(4)]
                if ASSOC_FIRST:
                    waiting[0:0] = jobs
                else:
                    waiting.extend(jobs)

        def after_a(gf, G):
            done_a.append((gf, G))
            if len([1 for f in range(4) if (f, G) in done_a]) == 4:
                waiting.extend([("r", 4 * G + j, n) for j in range(4) for n in range(2) if (4 * G + j, n) not in early])

        for s in range(10):
            now = units[s] if s < 8 else None
            prev = units[s - 1] if 1 <= s <= 8 else None
            old = units[s - 2] if s >= 2 else None
            fill = fills.get(s, [])
            for t in range(4):
                if now:
                    encode(now[0], now[1], t)
                if old and t == TQ[0]:
                    quant_b(*old)
                    after_b(*old)
                if old and t == TQ[1]:
                    quant_a(*old)
                    after_a(*old)
                if prev and t == 0:
                    relu(prev[0], prev[1], 1)
                for h in range(2):
                    if prev and t == TB[h]:
                        turn(prev[0], prev[1], h)
                for h in range(2):
                    if prev and t == TE[h]:
                        turn_out(prev[0], prev[1], h, "S")
                if prev and t == TI:
                    interleave_a(prev[0], prev[1], A_ROADS[s - 1])
                for k in range(t * len(fill) // 4, (t + 1) * len(fill) // 4):
                    fill[k]()
                if now:
                    drain(now[0], now[1], t)
                if now and t == 2:
                    relu(now[0], now[1], 0)
                if s == 8 and t == TP:
                    flush(100)
                    for k in range(EARLY):
                        early.append((4 * units[7][1] + k // 2, k % 2))
                        recon(early[k][0], early[k][1], 0, 3, "z")
                if s == 9 and t == TQ[1]:
                    for i, n in early:
                        recon(i, n, 3, 4)
                        recon_out(i, n, "SV"[turn_no[0] % 2])
                        turn_no[0] += 1
                if not (s == 8 and t >= TP):
                    flush(FLUSH[s] if now else 4)
        flush(100)
        for k in range(len(opened)):
            empty_one("SV"[k % 2])
